import numpy as np
import ml_dtypes


def mxq(x, axis, fmt="e4m3"):
    dtype, down = {"e4m3": (ml_dtypes.float8_e4m3fn, 7), "e5m2": (ml_dtypes.float8_e5m2, 14)}[fmt]
    v = np.moveaxis(np.asarray(x, np.float32).astype(ml_dtypes.bfloat16).astype(np.float64), axis, -1)
    blocks = v.reshape(v.shape[:-1] + (-1, 32))
    amax = np.abs(blocks).max(-1, keepdims=True)
    byte = np.maximum(np.where(amax > 0, np.frexp(amax)[1] - 1 + 127, 0) - down, 1)
    scale = np.exp2(byte - 127.0)
    codes = (blocks / scale).astype(np.float32).astype(dtype).astype(np.float64)
    return np.moveaxis((codes * scale).reshape(v.shape), -1, axis)


WIDE = False


def mx_kscale(k):
    if not WIDE:
        return np.ones(k)
    levels = np.array([10, -10, 5, -5, 0])
    if k % 512:
        return np.exp2(np.random.permutation(np.resize(levels, k // 32))).repeat(32)
    a = np.empty((k // 512, 16))
    for p in range(k // 512):
        a[p, :8] = np.random.permutation(np.resize(levels, 8))
        for g in range(8):
            far = levels[np.abs(levels - a[p, g]) >= 10]
            a[p, g + 8] = far[np.random.randint(len(far))]
    return np.exp2(a.ravel()).repeat(32)


def f64(x):
    return np.asarray(x).astype(np.float64)


def striped(idx):
    return np.tile(idx.reshape(-1, 16).T, (8, 1)).astype(np.uint16)


def unstriped(offs):
    return offs[:16].T.reshape(-1).astype(np.int64)


def striped8(idx):
    return np.concatenate([x.reshape(-1, 16).T for x in idx]).astype(np.uint16)


def runs(offs, k):
    lists = np.stack([offs[16 * r : 16 * r + 16].T.reshape(-1) for r in range(8)]).astype(np.int64)
    return lists[np.arange(k) % 512 // 64]


def pack_weight(w):
    k, n = w.shape
    w = f64(np.asarray(w, np.float32).astype(ml_dtypes.bfloat16)).reshape(k // 32, 32, n)
    amax = np.abs(w).max(1)
    byte = np.clip(np.where(amax > 0, np.frexp(amax)[1] - 1 + 127 - 7, 1), 1, 254)
    scaled = (w * np.exp2(127.0 - byte)[:, None, :]).reshape(k, n).astype(np.float32)
    words = np.ascontiguousarray(scaled.reshape(k // 512, 128, 4, n).transpose(0, 1, 3, 2)).astype(ml_dtypes.float8_e4m3fn).view(np.uint8)
    return words, np.ascontiguousarray(byte.astype(np.uint8).reshape(k // 512, 16, n))


def unpack_weight(words, scales):
    g, p, n, _ = words.shape
    vals = np.ascontiguousarray(words).view(ml_dtypes.float8_e4m3fn).astype(np.float64) * np.repeat(np.exp2(scales.astype(np.float64) - 127.0), 8, axis=1)[..., None]
    return vals.transpose(0, 1, 3, 2).reshape(g * 512, n)


def sigmoid(v):
    return 1.0 / (1.0 + np.exp(-np.maximum(v, -700.0)))


K, T, S, N, H, G = 512, 2048, 256, 512, 512, 2048


def setup_inputs():
    n = np.random.standard_normal
    s = mx_kscale(K)[:, None]
    u = mx_kscale(K)
    packed_xT = pack_weight(n((K, T)) * s)
    packed_dT = pack_weight(n((K, G)) / s)
    return {
        "x_words": packed_xT[0],
        "x_scales": packed_xT[1],
        "w1": (n((K, H)) / np.sqrt(K) / s).astype(np.float32),
        "gn": (np.random.uniform(0.5, 1.5, (H, 1)) * u[:, None]).astype(np.float32),
        "w2": (n((H, N)) / np.sqrt(H) / u[:, None]).astype(np.float32),
        "d_words": packed_dT[0],
        "d_scales": packed_dT[1],
        "offs": striped(np.random.permutation(T)[:S]),
        "n1": striped(np.random.permutation(S)),
        "n2": striped(np.random.permutation(S)),
        "two": striped(np.random.permutation(T)[:S]),
        "k1": striped8(np.random.randint(0, G, (8, H))),
        "n3": striped8(np.stack([np.random.permutation(S) for _ in range(8)])),
        "n4": striped8(np.stack([np.random.permutation(S) for _ in range(8)])),
    }


def reference(x_words, x_scales, w1, gn, w2, d_words, d_scales, offs, n1, n2, two, k1, n3, n4):
    xq = unpack_weight(x_words, x_scales)[:, unstriped(offs)]
    y = mxq(f64(w1), 0, "e4m3").T @ xq
    sm = np.maximum(y, y[:, unstriped(n2)])
    ds = np.zeros((H, S))
    ds[:, unstriped(n1)] = sm
    z = f64(gn) * (ds * sigmoid(y))
    a = mxq(f64(w2), 0, "e4m3").T @ mxq(z, 0, "e4m3")
    d_k1 = unpack_weight(d_words, d_scales)[np.arange(K)[:, None], runs(k1, K)]
    x_two = unpack_weight(x_words, x_scales)[:, unstriped(two)]
    b = 0.0625 * (d_k1.T @ x_two)
    return np.maximum(a, b[np.arange(H)[:, None], runs(n4, H)]) - (np.minimum(a[np.arange(N)[:, None], runs(n3, N)], b))

@@ -1,0 +1,189 @@
+from contextlib import ExitStack
+
+import concourse.mybir as mybir
+
+K, T, S, N, H, G = 512, 2048, 256, 512, 512, 2048
+FLOPS = 3 * 2 * K * H * S
+
+F32 = mybir.dt.float32
+BF16 = mybir.dt.bfloat16
+I32 = mybir.dt.int32
+U32 = mybir.dt.uint32
+U16 = mybir.dt.uint16
+U8 = mybir.dt.uint8
+FP8X4 = mybir.dt.float8_e4m3fn_x4
+ALU = mybir.AluOpType
+ACT = mybir.ActivationFunctionType
+
+P = 128
+PACK = 4
+
+
+def tile_picked_cdjoinmaxbsendg_none_p_kernel(
+    tc, x_words, x_scales, w1, gn, w2, d_words, d_scales, offs, n1, n2, two, k1, n3, n4, out
+):
+    nc = tc.nc
+    with ExitStack() as ctx:
+        keep = ctx.enter_context(tc.tile_pool(name="keep", bufs=1))
+        psum = ctx.enter_context(tc.psum_pool(name="psum", bufs=1))
+
+        def load_list(src, name):
+            t = keep.tile([P, src.shape[1]], U16, name=name)
+            nc.sync.dma_start(t[:], src)
+            return t
+
+        def load_words(src, name):
+            t = keep.tile([P, src.shape[2]], I32, name=name, align_bytes=64)
+            nc.sync.dma_start(t[:], src[0].rearrange("p n r -> p (n r)").bitcast(I32))
+            return t
+
+        def load_weight(src, name):
+            t = keep.tile([P, PACK, src.shape[1]], F32, name=name, tag=name, align_bytes=64)
+            nc.sync.dma_start(t[:], src.rearrange("(p j) c -> p j c", j=PACK))
+            return t
+
+        def gather(window, lst, dtype, name, tag=None):
+            t = keep.tile([P, 16 * lst.shape[1]], dtype, name=name, tag=tag or name, align_bytes=64)
+            nc.vector.tensor_copy(t[:], window.indirect(lst[:]))
+            return t
+
+        def round_and_deal(engine_copy, grouped, raw, m0, m1):
+            engine_copy(
+                grouped[:].rearrange("p t m j -> p m j t")[:, m0:m1],
+                raw[:].rearrange("p j (m t) -> p m j t", t=PACK),
+            )
+
+        def quantize(src, width, name):
+            codes = keep.tile([P, width], U32, name=name + "_codes", align_bytes=64)
+            scales = keep.tile([P, width], U8, name=name + "_scales", align_bytes=64)
+            nc.vector.quantize_mx(out=codes[:].bitcast(FP8X4), scales=scales[:], in_=src)
+            return codes, scales
+
+        def product(acc, lhs, t, rhs):
+            cols = slice(P * t, P * (t + 1))
+            nc.tensor.matmul_mx(
+                out=acc[:], lhsT=lhs[0][:, cols].bitcast(FP8X4), lhsT_scale=lhs[1][:, cols],
+                rhs=rhs[0][:].bitcast(FP8X4), rhs_scale=rhs[1][:], start=True, stop=True,
+            )
+
+        x_sc = keep.tile([P, T], U8, name="x_sc", align_bytes=64)
+        nc.vector.memset(x_sc[:].bitcast(I32), 0)
+        offs_t = load_list(offs, "offs_t")
+        two_t = load_list(two, "two_t")
+        w1_raw = [load_weight(w1[:, 256 * h : 256 * (h + 1)], "w1_raw%d" % h) for h in range(2)]
+        for q in range(4):
+            nc.sync.dma_start(x_sc[32 * q : 32 * q + 4, :].bitcast(I32), x_scales[0, 4 * q : 4 * q + 4, :].bitcast(I32))
+        k1_t = load_list(k1, "k1_t")
+        x_w = load_words(x_words, "x_w")
+        n2_t = load_list(n2, "n2_t")
+        d_sc = keep.tile([P, G], U8, name="d_sc", align_bytes=64)
+        nc.vector.memset(d_sc[:].bitcast(I32), 0)
+        for e in range(2):
+            nc.sync.dma_start(d_sc[e:P:16, :].bitcast(I32), d_scales[0, e:16:2, :].bitcast(I32))
+        n1_t = load_list(n1, "n1_t")
+        d_w = load_words(d_words, "d_w")
+        gn_t = keep.tile([P, PACK], F32, name="gn_t")
+        nc.sync.dma_start(gn_t[:], gn.rearrange("(p t) o -> p (t o)", t=PACK))
+        w2_raw = load_weight(w2, "w2_raw")
+        n4_t = load_list(n4, "n4_t")
+        n3_t = load_list(n3, "n3_t")
+
+        a_win = [keep.tile([P, 2 * S], F32, name="a_win%d" % t) for t in range(PACK)]
+        b_win = [keep.tile([P, 2 * S], F32, name="b_win%d" % t) for t in range(PACK)]
+        for win in a_win + b_win:
+            nc.vector.memset(win[:, S:], 0.0)
+
+        xs_offs = gather(x_sc[:], offs_t, U8, "xs_offs")
+        w1_g = keep.tile([P, PACK, P, PACK], BF16, name="w1_g", align_bytes=64)
+        for h in range(2):
+            round_and_deal(nc.vector.tensor_copy, w1_g, w1_raw[h], 64 * h, 64 * (h + 1))
+        w1_q = quantize(w1_g[:].rearrange("p t m j -> p (t m j)"), H, "w1")
+        xs_two = gather(x_sc[:], two_t, U8, "xs_two")
+        xw_offs = gather(x_w[:].bitcast(U32), offs_t, U32, "xw_offs", "xw")
+        ds_k1 = gather(d_sc[:], k1_t, U8, "ds_k1")
+        ds_placed = keep.tile([P, H], U8, name="ds_placed", tag="stage", align_bytes=64)
+        nc.vector.tensor_copy(ds_placed[:].bitcast(I32), ds_k1[:].bitcast(I32))
+        for e in range(2):
+            nc.sync.dma_start(ds_placed[2 + e : P : 32, :].bitcast(I32), ds_k1[16 + e : P : 32, :].bitcast(I32))
+
+        y_ps = [psum.tile([P, S], F32, name="y_ps%d" % t, tag="ya%d" % t) for t in range(PACK)]
+        y_win = [keep.tile([P, 2 * S], F32, name="y_win%d" % t) for t in range(PACK)]
+        ds_win = [keep.tile([P, 2 * S], F32, name="ds_win%d" % t) for t in range(PACK)]
+        for t in range(PACK):
+            product(y_ps[t], w1_q, t, (xw_offs, xs_offs))
+        for t in range(PACK):
+            nc.scalar.activation(y_win[t][:, S:], y_ps[t][:], ACT.Sigmoid)
+            nc.vector.tensor_copy(y_win[t][:, :S], y_ps[t][:])
+        def fetch_n2(t, tag):
+            got = keep.tile([P, S], F32, name="y_n2_%d" % t, tag=tag, align_bytes=64)
+            nc.scalar.activation(got[:], y_win[t][:].indirect(n2_t[:]), ACT.Copy)
+            return got
+
+        def larger(t, got, tag):
+            sm = keep.tile([P, S], F32, name="sm%d" % t, tag=tag, align_bytes=64)
+            nc.vector.tensor_tensor(sm[:], y_ps[t][:], got[:], ALU.max)
+            return sm
+
+        def send_n1(t, sm):
+            nc.scalar.activation(ds_win[t][:].indirect(n1_t[:]), sm[:], ACT.Copy)
+
+        got0 = fetch_n2(0, "got0")
+        sm0 = larger(0, got0, "sm0")
+        got1 = fetch_n2(1, "got1")
+        sm1 = larger(1, got1, "sm1")
+        send_n1(0, sm0)
+        got2 = fetch_n2(2, "sm0")
+        send_n1(1, sm1)
+        got3 = fetch_n2(3, "sm1")
+
+        xw_two = gather(x_w[:].bitcast(U32), two_t, U32, "xw_two", "got0")
+        dw_k1 = gather(d_w[:].bitcast(U32), k1_t, U32, "dw_k1", "got1")
+        d_codes = keep.tile([P, H], U32, name="d_codes", align_bytes=64)
+        nc.vector.tensor_copy(d_codes[:].rearrange("p (t m) -> p m t", t=PACK), dw_k1[:].rearrange("p (m t) -> p m t", t=PACK))
+        sm2 = larger(2, got2, "got1")
+        send_n1(2, sm2)
+        d_bytes = keep.tile([P, H], U8, name="d_bytes", tag="sm0", align_bytes=64)
+        nc.vector.tensor_copy(d_bytes[:].rearrange("p (t m) -> p m t", t=PACK), ds_placed[:].rearrange("p (m t) -> p m t", t=PACK))
+        w2_g = keep.tile([P, PACK, P, PACK], BF16, name="w2_g", tag="stage", align_bytes=64)
+        round_and_deal(nc.vector.tensor_copy, w2_g, w2_raw, 0, 128)
+        sm3 = larger(3, got3, "w2_raw")
+        send_n1(3, sm3)
+        b_ps = [psum.tile([P, S], F32, name="b_ps%d" % t) for t in range(PACK)]
+        for t in range(PACK):
+            product(b_ps[t], (d_codes, d_bytes), t, (xw_two, xs_two))
+        for t in range(PACK):
+            nc.vector.tensor_scalar(b_win[t][:, :S], b_ps[t][:], 0.0625, None, ALU.mult)
+
+        w2_q = quantize(w2_g[:].rearrange("p t m j -> p (t m j)"), N, "w2")
+
+        z_planes = keep.tile([P, PACK, S], BF16, name="z_planes", tag="stage", align_bytes=64)
+        for t in range(PACK):
+            nc.vector.scalar_tensor_tensor(
+                z_planes[:, t, :], ds_win[t][:, :S], gn_t[:, t : t + 1], y_win[t][:, S:], ALU.mult, ALU.mult
+            )
+        z_g = keep.tile([P, S, PACK], BF16, name="z_g", align_bytes=64)
+        nc.vector.tensor_copy(z_g[:], z_planes[:].rearrange("p t s -> p s t"))
+        z_q = quantize(z_g[:].rearrange("p s t -> p (s t)"), S, "z")
+
+        b_n4 = keep.tile([P, PACK, S], F32, name="b_n4", tag="w2_raw", align_bytes=64)
+        for t in range(PACK):
+            nc.scalar.activation(b_n4[:, t, :], b_win[t][:].indirect(n4_t[:]), ACT.Copy)
+
+        a_ps = [psum.tile([P, S], F32, name="a_ps%d" % t, tag="ya%d" % t) for t in range(PACK)]
+        for t in range(PACK):
+            product(a_ps[t], w2_q, t, z_q)
+        a_n3 = keep.tile([P, PACK, S], F32, name="a_n3")
+        hi = keep.tile([P, PACK, S], F32, name="hi")
+        lo = keep.tile([P, PACK, S], F32, name="lo")
+        res = keep.tile([P, PACK, S], F32, name="res")
+        out_v = out.rearrange("(p t) j -> p t j", t=PACK)
+        for t in range(PACK):
+            if t == 0:
+                nc.vector.tensor_copy(a_win[t][:, :S], a_ps[t][:])
+            else:
+                nc.scalar.copy(a_win[t][:, :S], a_ps[t][:])
+            nc.scalar.activation(a_n3[:, t, :], a_win[t][:].indirect(n3_t[:]), ACT.Copy)
+            nc.vector.tensor_tensor(hi[:, t, :], a_ps[t][:], b_n4[:, t, :], ALU.max)
+            nc.vector.tensor_tensor(lo[:, t, :], a_n3[:, t, :], b_win[t][:, :S], ALU.min)
+            nc.vector.tensor_tensor(res[:, t, :], hi[:, t, :], lo[:, t, :], ALU.subtract)
+            nc.sync.dma_start(out_v[:, t, :], res[:, t, :])

@@ -49,12 +49,12 @@ def tile_picked_cdjoinmaxbsendg_none_p_kernel(
 
         def round_and_deal(engine_copy, grouped, raw, m0, m1):
             engine_copy(
-                grouped[:].rearrange("p t m j -> p m j t")[:, m0:m1],
-                raw[:].rearrange("p j (m t) -> p m j t", t=PACK),
+                grouped[:].rearrange("p t m j -> p m t j")[:, m0:m1],
+                raw[:].rearrange("p j (m t) -> p m t j", t=PACK),
             )
 
-        def quantize(src, width, name):
-            codes = keep.tile([P, width], U32, name=name + "_codes", align_bytes=64)
+        def quantize(src, width, name, tag=None):
+            codes = keep.tile([P, width], U32, name=name + "_codes", tag=tag or name, align_bytes=64)
             scales = keep.tile([P, width], U8, name=name + "_scales", align_bytes=64)
             nc.vector.quantize_mx(out=codes[:].bitcast(FP8X4), scales=scales[:], in_=src)
             return codes, scales
@@ -62,24 +62,25 @@ def tile_picked_cdjoinmaxbsendg_none_p_kernel(
         def product(acc, lhs, t, rhs):
             cols = slice(P * t, P * (t + 1))
             nc.tensor.matmul_mx(
-                out=acc[:], lhsT=lhs[0][:, cols].bitcast(FP8X4), lhsT_scale=lhs[1][:, cols],
+                out=acc, lhsT=lhs[0][:, cols].bitcast(FP8X4), lhsT_scale=lhs[1][:, cols],
                 rhs=rhs[0][:].bitcast(FP8X4), rhs_scale=rhs[1][:], start=True, stop=True,
             )
 
         x_sc = keep.tile([P, T], U8, name="x_sc", align_bytes=64)
         nc.vector.memset(x_sc[:].bitcast(I32), 0)
-        offs_t = load_list(offs, "offs_t")
-        two_t = load_list(two, "two_t")
-        w1_raw = [load_weight(w1[:, 256 * h : 256 * (h + 1)], "w1_raw%d" % h) for h in range(2)]
-        for q in range(4):
-            nc.sync.dma_start(x_sc[32 * q : 32 * q + 4, :].bitcast(I32), x_scales[0, 4 * q : 4 * q + 4, :].bitcast(I32))
-        k1_t = load_list(k1, "k1_t")
-        x_w = load_words(x_words, "x_w")
-        n2_t = load_list(n2, "n2_t")
         d_sc = keep.tile([P, G], U8, name="d_sc", align_bytes=64)
         nc.vector.memset(d_sc[:].bitcast(I32), 0)
+        offs_t = load_list(offs, "offs_t")
+        k1_t = load_list(k1, "k1_t")
+        two_t = load_list(two, "two_t")
+        w1_raw = [load_weight(w1[:, :256], "w1_raw0")]
+        for q in range(4):
+            nc.sync.dma_start(x_sc[32 * q : 32 * q + 4, :].bitcast(I32), x_scales[0, 4 * q : 4 * q + 4, :].bitcast(I32))
         for e in range(2):
             nc.sync.dma_start(d_sc[e:P:16, :].bitcast(I32), d_scales[0, e:16:2, :].bitcast(I32))
+        w1_raw.append(load_weight(w1[:, 256:], "w1_raw1"))
+        x_w = load_words(x_words, "x_w")
+        n2_t = load_list(n2, "n2_t")
         n1_t = load_list(n1, "n1_t")
         d_w = load_words(d_words, "d_w")
         gn_t = keep.tile([P, PACK], F32, name="gn_t")
@@ -93,24 +94,27 @@ def tile_picked_cdjoinmaxbsendg_none_p_kernel(
         for win in a_win + b_win:
             nc.vector.memset(win[:, S:], 0.0)
 
+        warm = keep.tile([P, 1], F32, name="warm")
+        nc.scalar.activation(warm[:], a_win[0][:, S : S + 1], ACT.Sigmoid)
         xs_offs = gather(x_sc[:], offs_t, U8, "xs_offs")
-        w1_g = keep.tile([P, PACK, P, PACK], BF16, name="w1_g", align_bytes=64)
-        for h in range(2):
-            round_and_deal(nc.vector.tensor_copy, w1_g, w1_raw[h], 64 * h, 64 * (h + 1))
-        w1_q = quantize(w1_g[:].rearrange("p t m j -> p (t m j)"), H, "w1")
         xs_two = gather(x_sc[:], two_t, U8, "xs_two")
-        xw_offs = gather(x_w[:].bitcast(U32), offs_t, U32, "xw_offs", "xw")
         ds_k1 = gather(d_sc[:], k1_t, U8, "ds_k1")
-        ds_placed = keep.tile([P, H], U8, name="ds_placed", tag="stage", align_bytes=64)
+        ds_placed = keep.tile([P, H], U8, name="ds_placed", tag="placed", align_bytes=64)
         nc.vector.tensor_copy(ds_placed[:].bitcast(I32), ds_k1[:].bitcast(I32))
         for e in range(2):
             nc.sync.dma_start(ds_placed[2 + e : P : 32, :].bitcast(I32), ds_k1[16 + e : P : 32, :].bitcast(I32))
+        w1_g = keep.tile([P, PACK, P, PACK], BF16, name="w1_g", tag="xw", align_bytes=64)
+        round_and_deal(nc.scalar.copy, w1_g, w1_raw[0], 0, 64)
+        round_and_deal(nc.scalar.copy, w1_g, w1_raw[1], 64, 128)
+        w1_q = quantize(w1_g[:].rearrange("p t m j -> p (t m j)"), H, "w1")
+        xw_offs = gather(x_w[:].bitcast(U32), offs_t, U32, "xw_offs", "xw")
+        xw_two = gather(x_w[:].bitcast(U32), two_t, U32, "xw_two")
 
         y_ps = [psum.tile([P, S], F32, name="y_ps%d" % t, tag="ya%d" % t) for t in range(PACK)]
         y_win = [keep.tile([P, 2 * S], F32, name="y_win%d" % t) for t in range(PACK)]
         ds_win = [keep.tile([P, 2 * S], F32, name="ds_win%d" % t) for t in range(PACK)]
         for t in range(PACK):
-            product(y_ps[t], w1_q, t, (xw_offs, xs_offs))
+            product(y_ps[t][:], w1_q, t, (xw_offs, xs_offs))
         for t in range(PACK):
             nc.scalar.activation(y_win[t][:, S:], y_ps[t][:], ACT.Sigmoid)
             nc.vector.tensor_copy(y_win[t][:, :S], y_ps[t][:])
@@ -127,63 +131,66 @@ def tile_picked_cdjoinmaxbsendg_none_p_kernel(
         def send_n1(t, sm):
             nc.scalar.activation(ds_win[t][:].indirect(n1_t[:]), sm[:], ACT.Copy)
 
-        got0 = fetch_n2(0, "got0")
-        sm0 = larger(0, got0, "sm0")
-        got1 = fetch_n2(1, "got1")
-        sm1 = larger(1, got1, "sm1")
-        send_n1(0, sm0)
-        got2 = fetch_n2(2, "sm0")
-        send_n1(1, sm1)
-        got3 = fetch_n2(3, "sm1")
-
-        xw_two = gather(x_w[:].bitcast(U32), two_t, U32, "xw_two", "got0")
+        got = [fetch_n2(t, "got%d" % t) for t in range(PACK)]
+        send_n1(0, larger(0, got[0], "sm0"))
+        send_n1(1, larger(1, got[1], "sm1"))
         dw_k1 = gather(d_w[:].bitcast(U32), k1_t, U32, "dw_k1", "got1")
         d_codes = keep.tile([P, H], U32, name="d_codes", align_bytes=64)
         nc.vector.tensor_copy(d_codes[:].rearrange("p (t m) -> p m t", t=PACK), dw_k1[:].rearrange("p (m t) -> p m t", t=PACK))
-        sm2 = larger(2, got2, "got1")
-        send_n1(2, sm2)
-        d_bytes = keep.tile([P, H], U8, name="d_bytes", tag="sm0", align_bytes=64)
-        nc.vector.tensor_copy(d_bytes[:].rearrange("p (t m) -> p m t", t=PACK), ds_placed[:].rearrange("p (m t) -> p m t", t=PACK))
+        send_n1(2, larger(2, got[2], "sm2"))
+        send_n1(3, larger(3, got[3], "got1"))
         w2_g = keep.tile([P, PACK, P, PACK], BF16, name="w2_g", tag="stage", align_bytes=64)
         round_and_deal(nc.vector.tensor_copy, w2_g, w2_raw, 0, 128)
-        sm3 = larger(3, got3, "w2_raw")
-        send_n1(3, sm3)
+        d_bytes = keep.tile([P, H], U8, name="d_bytes", tag="w2_raw", align_bytes=64)
+        nc.vector.tensor_copy(d_bytes[:].rearrange("p (t m) -> p t m", t=PACK), ds_placed[:].rearrange("p (m t) -> p t m", t=PACK))
         b_ps = [psum.tile([P, S], F32, name="b_ps%d" % t) for t in range(PACK)]
         for t in range(PACK):
-            product(b_ps[t], (d_codes, d_bytes), t, (xw_two, xs_two))
+            product(b_ps[t][:], (d_codes, d_bytes), t, (xw_two, xs_two))
         for t in range(PACK):
             nc.vector.tensor_scalar(b_win[t][:, :S], b_ps[t][:], 0.0625, None, ALU.mult)
 
-        w2_q = quantize(w2_g[:].rearrange("p t m j -> p (t m j)"), N, "w2")
+        w2_q = quantize(w2_g[:].rearrange("p t m j -> p (t m j)"), N, "w2", "placed")
 
-        z_planes = keep.tile([P, PACK, S], BF16, name="z_planes", tag="stage", align_bytes=64)
-        for t in range(PACK):
+        HALF = S // 2
+        z_planes = keep.tile([P, PACK, S], F32, name="z_planes", tag="stage", align_bytes=64)
+
+        def z_plane(t, cols):
             nc.vector.scalar_tensor_tensor(
-                z_planes[:, t, :], ds_win[t][:, :S], gn_t[:, t : t + 1], y_win[t][:, S:], ALU.mult, ALU.mult
+                z_planes[:, t, cols], ds_win[t][:, cols], gn_t[:, t : t + 1], y_win[t][:, S:][:, cols], ALU.mult, ALU.mult
             )
-        z_g = keep.tile([P, S, PACK], BF16, name="z_g", align_bytes=64)
-        nc.vector.tensor_copy(z_g[:], z_planes[:].rearrange("p t s -> p s t"))
-        z_q = quantize(z_g[:].rearrange("p s t -> p (s t)"), S, "z")
 
-        b_n4 = keep.tile([P, PACK, S], F32, name="b_n4", tag="w2_raw", align_bytes=64)
+        halves = [slice(HALF * h, HALF * (h + 1)) for h in range(2)]
+        for t in range(PACK - 1):
+            z_plane(t, slice(0, S))
+        for cols in halves:
+            z_plane(PACK - 1, cols)
+        z_g = [keep.tile([P, HALF, PACK], BF16, name="z_g%d" % h, align_bytes=64) for h in range(2)]
+        for h in range(2):
+            nc.vector.tensor_copy(z_g[h][:], z_planes[:, :, halves[h]].rearrange("p t s -> p s t"))
+        z_q = [quantize(z_g[h][:].rearrange("p s t -> p (s t)"), HALF, "z%d" % h) for h in range(2)]
+
+        b_n4 = keep.tile([P, PACK, S], F32, name="b_n4", tag="got1", align_bytes=64)
         for t in range(PACK):
             nc.scalar.activation(b_n4[:, t, :], b_win[t][:].indirect(n4_t[:]), ACT.Copy)
 
         a_ps = [psum.tile([P, S], F32, name="a_ps%d" % t, tag="ya%d" % t) for t in range(PACK)]
         for t in range(PACK):
-            product(a_ps[t], w2_q, t, z_q)
+            for h in range(2):
+                product(a_ps[t][:, halves[h]], w2_q, t, z_q[h])
         a_n3 = keep.tile([P, PACK, S], F32, name="a_n3")
         hi = keep.tile([P, PACK, S], F32, name="hi")
         lo = keep.tile([P, PACK, S], F32, name="lo")
         res = keep.tile([P, PACK, S], F32, name="res")
         out_v = out.rearrange("(p t) j -> p t j", t=PACK)
         for t in range(PACK):
-            if t == 0:
-                nc.vector.tensor_copy(a_win[t][:, :S], a_ps[t][:])
-            else:
+            if t == 1:
                 nc.scalar.copy(a_win[t][:, :S], a_ps[t][:])
+            else:
+                nc.vector.tensor_copy(a_win[t][:, :S], a_ps[t][:])
+        for t in range(PACK):
             nc.scalar.activation(a_n3[:, t, :], a_win[t][:].indirect(n3_t[:]), ACT.Copy)
             nc.vector.tensor_tensor(hi[:, t, :], a_ps[t][:], b_n4[:, t, :], ALU.max)
-            nc.vector.tensor_tensor(lo[:, t, :], a_n3[:, t, :], b_win[t][:, :S], ALU.min)
-            nc.vector.tensor_tensor(res[:, t, :], hi[:, t, :], lo[:, t, :], ALU.subtract)
+            nc.vector.scalar_tensor_tensor(lo[:, t, :], b_ps[t][:], 0.0625, a_n3[:, t, :], ALU.mult, ALU.min)
+            last = nc.vector if t == PACK - 1 else nc.gpsimd
+            last.tensor_tensor(res[:, t, :], hi[:, t, :], lo[:, t, :], ALU.subtract)
             nc.sync.dma_start(out_v[:, t, :], res[:, t, :])

@@ -47,10 +47,10 @@ def tile_picked_cdjoinmaxbsendg_none_p_kernel(
             nc.vector.tensor_copy(t[:], window.indirect(lst[:]))
             return t
 
-        def round_and_deal(engine_copy, grouped, raw, m0, m1):
+        def round_and_deal(engine_copy, grouped, raw, m0, m1, first=0):
             engine_copy(
                 grouped[:].rearrange("p t m j -> p m t j")[:, m0:m1],
-                raw[:].rearrange("p j (m t) -> p m t j", t=PACK),
+                raw[:].rearrange("p j (m t) -> p m t j", t=PACK)[:, m0 - first : m1 - first],
             )
 
         def quantize(src, width, name, tag=None):
@@ -59,10 +59,10 @@ def tile_picked_cdjoinmaxbsendg_none_p_kernel(
             nc.vector.quantize_mx(out=codes[:].bitcast(FP8X4), scales=scales[:], in_=src)
             return codes, scales
 
-        def product(acc, lhs, t, rhs):
+        def product(acc, lhs, t, rhs, row0=0):
             cols = slice(P * t, P * (t + 1))
             nc.tensor.matmul_mx(
-                out=acc, lhsT=lhs[0][:, cols].bitcast(FP8X4), lhsT_scale=lhs[1][:, cols],
+                out=acc, lhsT=lhs[0][:, cols].bitcast(FP8X4), lhsT_scale=lhs[1][row0:, cols],
                 rhs=rhs[0][:].bitcast(FP8X4), rhs_scale=rhs[1][:], start=True, stop=True,
             )
 
@@ -72,15 +72,15 @@ def tile_picked_cdjoinmaxbsendg_none_p_kernel(
         nc.vector.memset(d_sc[:].bitcast(I32), 0)
         offs_t = load_list(offs, "offs_t")
         k1_t = load_list(k1, "k1_t")
-        two_t = load_list(two, "two_t")
+        n2_t = load_list(n2, "n2_t")
         w1_raw = [load_weight(w1[:, :256], "w1_raw0")]
         for q in range(4):
             nc.sync.dma_start(x_sc[32 * q : 32 * q + 4, :].bitcast(I32), x_scales[0, 4 * q : 4 * q + 4, :].bitcast(I32))
         for e in range(2):
-            nc.sync.dma_start(d_sc[e:P:16, :].bitcast(I32), d_scales[0, e:16:2, :].bitcast(I32))
+            nc.sync.dma_start(d_sc[8 + e : P : 16, :].bitcast(I32), d_scales[0, e:16:2, :].bitcast(I32))
         w1_raw.append(load_weight(w1[:, 256:], "w1_raw1"))
         x_w = load_words(x_words, "x_w")
-        n2_t = load_list(n2, "n2_t")
+        two_t = load_list(two, "two_t")
         n1_t = load_list(n1, "n1_t")
         d_w = load_words(d_words, "d_w")
         gn_t = keep.tile([P, PACK], F32, name="gn_t")
@@ -96,18 +96,19 @@ def tile_picked_cdjoinmaxbsendg_none_p_kernel(
 
         warm = keep.tile([P, 1], F32, name="warm")
         nc.scalar.activation(warm[:], a_win[0][:, S : S + 1], ACT.Sigmoid)
+        w1_g = keep.tile([P, PACK, P, PACK], BF16, name="w1_g", tag="xw", align_bytes=64)
+        round_and_deal(nc.scalar.copy, w1_g, w1_raw[0], 0, 64)
+        round_and_deal(nc.scalar.copy, w1_g, w1_raw[1], 64, 96, 64)
         xs_offs = gather(x_sc[:], offs_t, U8, "xs_offs")
-        xs_two = gather(x_sc[:], two_t, U8, "xs_two")
         ds_k1 = gather(d_sc[:], k1_t, U8, "ds_k1")
         ds_placed = keep.tile([P, H], U8, name="ds_placed", tag="placed", align_bytes=64)
         nc.vector.tensor_copy(ds_placed[:].bitcast(I32), ds_k1[:].bitcast(I32))
         for e in range(2):
-            nc.sync.dma_start(ds_placed[2 + e : P : 32, :].bitcast(I32), ds_k1[16 + e : P : 32, :].bitcast(I32))
-        w1_g = keep.tile([P, PACK, P, PACK], BF16, name="w1_g", tag="xw", align_bytes=64)
-        round_and_deal(nc.scalar.copy, w1_g, w1_raw[0], 0, 64)
-        round_and_deal(nc.scalar.copy, w1_g, w1_raw[1], 64, 128)
+            nc.sync.dma_start(ds_placed[10 + e : P : 32, :].bitcast(I32), ds_k1[24 + e : P : 32, :].bitcast(I32))
+        round_and_deal(nc.vector.tensor_copy, w1_g, w1_raw[1], 96, 128, 64)
         w1_q = quantize(w1_g[:].rearrange("p t m j -> p (t m j)"), H, "w1")
         xw_offs = gather(x_w[:].bitcast(U32), offs_t, U32, "xw_offs", "xw")
+        xs_two = gather(x_sc[:], two_t, U8, "xs_two")
         xw_two = gather(x_w[:].bitcast(U32), two_t, U32, "xw_two")
 
         y_ps = [psum.tile([P, S], F32, name="y_ps%d" % t, tag="ya%d" % t) for t in range(PACK)]
@@ -145,7 +146,7 @@ def tile_picked_cdjoinmaxbsendg_none_p_kernel(
         nc.vector.tensor_copy(d_bytes[:].rearrange("p (t m) -> p t m", t=PACK), ds_placed[:].rearrange("p (m t) -> p t m", t=PACK))
         b_ps = [psum.tile([P, S], F32, name="b_ps%d" % t) for t in range(PACK)]
         for t in range(PACK):
-            product(b_ps[t][:], (d_codes, d_bytes), t, (xw_two, xs_two))
+            product(b_ps[t][:], (d_codes, d_bytes), t, (xw_two, xs_two), 8)
         for t in range(PACK):
             nc.vector.tensor_scalar(b_win[t][:, :S], b_ps[t][:], 0.0625, None, ALU.mult)
 
@@ -167,7 +168,12 @@ def tile_picked_cdjoinmaxbsendg_none_p_kernel(
         z_g = [keep.tile([P, HALF, PACK], BF16, name="z_g%d" % h, align_bytes=64) for h in range(2)]
         for h in range(2):
             nc.vector.tensor_copy(z_g[h][:], z_planes[:, :, halves[h]].rearrange("p t s -> p s t"))
-        z_q = [quantize(z_g[h][:].rearrange("p s t -> p (s t)"), HALF, "z%d" % h) for h in range(2)]
+        z_codes = keep.tile([P, S], U32, name="z_codes", align_bytes=64)
+        z_scales = keep.tile([P, S], U8, name="z_scales", align_bytes=64)
+        for h in range(2):
+            nc.vector.quantize_mx(
+                out=z_codes[:, halves[h]].bitcast(FP8X4), scales=z_scales[:, halves[h]], in_=z_g[h][:].rearrange("p s t -> p (s t)")
+            )
 
         b_n4 = keep.tile([P, PACK, S], F32, name="b_n4", tag="got1", align_bytes=64)
         for t in range(PACK):
@@ -175,22 +181,33 @@ def tile_picked_cdjoinmaxbsendg_none_p_kernel(
 
         a_ps = [psum.tile([P, S], F32, name="a_ps%d" % t, tag="ya%d" % t) for t in range(PACK)]
         for t in range(PACK):
-            for h in range(2):
-                product(a_ps[t][:, halves[h]], w2_q, t, z_q[h])
+            product(a_ps[t][:], w2_q, t, (z_codes, z_scales))
         a_n3 = keep.tile([P, PACK, S], F32, name="a_n3")
         hi = keep.tile([P, PACK, S], F32, name="hi")
         lo = keep.tile([P, PACK, S], F32, name="lo")
         res = keep.tile([P, PACK, S], F32, name="res")
         out_v = out.rearrange("(p t) j -> p t j", t=PACK)
         for t in range(PACK):
-            if t == 1:
-                nc.scalar.copy(a_win[t][:, :S], a_ps[t][:])
-            else:
-                nc.vector.tensor_copy(a_win[t][:, :S], a_ps[t][:])
-        for t in range(PACK):
-            nc.scalar.activation(a_n3[:, t, :], a_win[t][:].indirect(n3_t[:]), ACT.Copy)
+            nc.vector.tensor_copy(a_win[t][:, :S], a_ps[t][:])
+
+        def fetch_n3(t, cols):
+            entries = n3_t[:, cols.start // 16 : cols.stop // 16]
+            nc.scalar.activation(a_n3[:, t, cols], a_win[t][:].indirect(entries), ACT.Copy)
+
+        def smaller(t, cols):
+            nc.vector.scalar_tensor_tensor(lo[:, t, cols], b_ps[t][:, cols], 0.0625, a_n3[:, t, cols], ALU.mult, ALU.min)
+
+        for t in range(PACK - 1):
+            fetch_n3(t, slice(0, S))
             nc.vector.tensor_tensor(hi[:, t, :], a_ps[t][:], b_n4[:, t, :], ALU.max)
-            nc.vector.scalar_tensor_tensor(lo[:, t, :], b_ps[t][:], 0.0625, a_n3[:, t, :], ALU.mult, ALU.min)
-            last = nc.vector if t == PACK - 1 else nc.gpsimd
-            last.tensor_tensor(res[:, t, :], hi[:, t, :], lo[:, t, :], ALU.subtract)
+            smaller(t, slice(0, S))
+            nc.vector.tensor_tensor(res[:, t, :], hi[:, t, :], lo[:, t, :], ALU.subtract)
             nc.sync.dma_start(out_v[:, t, :], res[:, t, :])
+        t = PACK - 1
+        nc.vector.tensor_tensor(hi[:, t, :], a_ps[t][:], b_n4[:, t, :], ALU.max)
+        for cols in halves:
+            fetch_n3(t, cols)
+            smaller(t, cols)
+        for cols in halves:
+            nc.vector.tensor_tensor(res[:, t, cols], hi[:, t, cols], lo[:, t, cols], ALU.subtract)
+        nc.sync.dma_start(out_v[:, t, :], res[:, t, :])

from contextlib import ExitStack

import concourse.mybir as mybir

K, T, S, N, H, G = 512, 2048, 256, 512, 512, 2048
FLOPS = 3 * 2 * K * H * S

F32 = mybir.dt.float32
BF16 = mybir.dt.bfloat16
I32 = mybir.dt.int32
U32 = mybir.dt.uint32
U16 = mybir.dt.uint16
U8 = mybir.dt.uint8
FP8X4 = mybir.dt.float8_e4m3fn_x4
ALU = mybir.AluOpType
ACT = mybir.ActivationFunctionType

P = 128
PACK = 4


def tile_picked_cdjoinmaxbsendg_none_p_kernel(
    tc, x_words, x_scales, w1, gn, w2, d_words, d_scales, offs, n1, n2, two, k1, n3, n4, out
):
    nc = tc.nc
    with ExitStack() as ctx:
        keep = ctx.enter_context(tc.tile_pool(name="keep", bufs=1))
        psum = ctx.enter_context(tc.psum_pool(name="psum", bufs=1))

        def load_list(src, name):
            t = keep.tile([P, src.shape[1]], U16, name=name)
            nc.sync.dma_start(t[:], src)
            return t

        def load_words(src, name):
            t = keep.tile([P, src.shape[2]], I32, name=name, align_bytes=64)
            nc.sync.dma_start(t[:], src[0].rearrange("p n r -> p (n r)").bitcast(I32))
            return t

        def load_weight(src, name):
            t = keep.tile([P, PACK, src.shape[1]], F32, name=name, tag=name, align_bytes=64)
            nc.sync.dma_start(t[:], src.rearrange("(p j) c -> p j c", j=PACK))
            return t

        def gather(window, lst, dtype, name, tag=None):
            t = keep.tile([P, 16 * lst.shape[1]], dtype, name=name, tag=tag or name, align_bytes=64)
            nc.vector.tensor_copy(t[:], window.indirect(lst[:]))
            return t

        def round_and_deal(engine_copy, grouped, raw, m0, m1, first=0):
            engine_copy(
                grouped[:].rearrange("p t m j -> p m t j")[:, m0:m1],
                raw[:].rearrange("p j (m t) -> p m t j", t=PACK)[:, m0 - first : m1 - first],
            )

        def quantize(src, width, name, tag=None):
            codes = keep.tile([P, width], U32, name=name + "_codes", tag=tag or name, align_bytes=64)
            scales = keep.tile([P, width], U8, name=name + "_scales", align_bytes=64)
            nc.vector.quantize_mx(out=codes[:].bitcast(FP8X4), scales=scales[:], in_=src)
            return codes, scales

        def product(acc, lhs, t, rhs, row0=0):
            cols = slice(P * t, P * (t + 1))
            nc.tensor.matmul_mx(
                out=acc, lhsT=lhs[0][:, cols].bitcast(FP8X4), lhsT_scale=lhs[1][row0:, cols],
                rhs=rhs[0][:].bitcast(FP8X4), rhs_scale=rhs[1][:], start=True, stop=True,
            )

        x_sc = keep.tile([P, T], U8, name="x_sc", align_bytes=64)
        nc.vector.memset(x_sc[:].bitcast(I32), 0)
        d_sc = keep.tile([P, G], U8, name="d_sc", align_bytes=64)
        nc.vector.memset(d_sc[:].bitcast(I32), 0)
        offs_t = load_list(offs, "offs_t")
        k1_t = load_list(k1, "k1_t")
        n2_t = load_list(n2, "n2_t")
        w1_raw = [load_weight(w1[:, :256], "w1_raw0")]
        for q in range(4):
            nc.sync.dma_start(x_sc[32 * q : 32 * q + 4, :].bitcast(I32), x_scales[0, 4 * q : 4 * q + 4, :].bitcast(I32))
        for e in range(2):
            nc.sync.dma_start(d_sc[8 + e : P : 16, :].bitcast(I32), d_scales[0, e:16:2, :].bitcast(I32))
        w1_raw.append(load_weight(w1[:, 256:], "w1_raw1"))
        x_w = load_words(x_words, "x_w")
        two_t = load_list(two, "two_t")
        n1_t = load_list(n1, "n1_t")
        d_w = load_words(d_words, "d_w")
        gn_t = keep.tile([P, PACK], F32, name="gn_t")
        nc.sync.dma_start(gn_t[:], gn.rearrange("(p t) o -> p (t o)", t=PACK))
        w2_raw = load_weight(w2, "w2_raw")
        n4_t = load_list(n4, "n4_t")
        n3_t = load_list(n3, "n3_t")

        a_win = [keep.tile([P, 2 * S], F32, name="a_win%d" % t) for t in range(PACK)]
        b_win = [keep.tile([P, 2 * S], F32, name="b_win%d" % t) for t in range(PACK)]
        for win in a_win + b_win:
            nc.vector.memset(win[:, S:], 0.0)

        warm = keep.tile([P, 1], F32, name="warm")
        nc.scalar.activation(warm[:], a_win[0][:, S : S + 1], ACT.Sigmoid)
        w1_g = keep.tile([P, PACK, P, PACK], BF16, name="w1_g", tag="xw", align_bytes=64)
        round_and_deal(nc.scalar.copy, w1_g, w1_raw[0], 0, 64)
        round_and_deal(nc.scalar.copy, w1_g, w1_raw[1], 64, 96, 64)
        xs_offs = gather(x_sc[:], offs_t, U8, "xs_offs")
        ds_k1 = gather(d_sc[:], k1_t, U8, "ds_k1")
        ds_placed = keep.tile([P, H], U8, name="ds_placed", tag="placed", align_bytes=64)
        nc.vector.tensor_copy(ds_placed[:].bitcast(I32), ds_k1[:].bitcast(I32))
        for e in range(2):
            nc.sync.dma_start(ds_placed[10 + e : P : 32, :].bitcast(I32), ds_k1[24 + e : P : 32, :].bitcast(I32))
        round_and_deal(nc.vector.tensor_copy, w1_g, w1_raw[1], 96, 128, 64)
        w1_q = quantize(w1_g[:].rearrange("p t m j -> p (t m j)"), H, "w1")
        xw_offs = gather(x_w[:].bitcast(U32), offs_t, U32, "xw_offs", "xw")
        xs_two = gather(x_sc[:], two_t, U8, "xs_two")
        xw_two = gather(x_w[:].bitcast(U32), two_t, U32, "xw_two")

        y_ps = [psum.tile([P, S], F32, name="y_ps%d" % t, tag="ya%d" % t) for t in range(PACK)]
        y_win = [keep.tile([P, 2 * S], F32, name="y_win%d" % t) for t in range(PACK)]
        ds_win = [keep.tile([P, 2 * S], F32, name="ds_win%d" % t) for t in range(PACK)]
        for t in range(PACK):
            product(y_ps[t][:], w1_q, t, (xw_offs, xs_offs))
        for t in range(PACK):
            nc.scalar.activation(y_win[t][:, S:], y_ps[t][:], ACT.Sigmoid)
            nc.vector.tensor_copy(y_win[t][:, :S], y_ps[t][:])
        def fetch_n2(t, tag):
            got = keep.tile([P, S], F32, name="y_n2_%d" % t, tag=tag, align_bytes=64)
            nc.scalar.activation(got[:], y_win[t][:].indirect(n2_t[:]), ACT.Copy)
            return got

        def larger(t, got, tag):
            sm = keep.tile([P, S], F32, name="sm%d" % t, tag=tag, align_bytes=64)
            nc.vector.tensor_tensor(sm[:], y_ps[t][:], got[:], ALU.max)
            return sm

        def send_n1(t, sm):
            nc.scalar.activation(ds_win[t][:].indirect(n1_t[:]), sm[:], ACT.Copy)

        got = [fetch_n2(t, "got%d" % t) for t in range(PACK)]
        send_n1(0, larger(0, got[0], "sm0"))
        send_n1(1, larger(1, got[1], "sm1"))
        dw_k1 = gather(d_w[:].bitcast(U32), k1_t, U32, "dw_k1", "got1")
        d_codes = keep.tile([P, H], U32, name="d_codes", align_bytes=64)
        nc.vector.tensor_copy(d_codes[:].rearrange("p (t m) -> p m t", t=PACK), dw_k1[:].rearrange("p (m t) -> p m t", t=PACK))
        send_n1(2, larger(2, got[2], "sm2"))
        send_n1(3, larger(3, got[3], "got1"))
        w2_g = keep.tile([P, PACK, P, PACK], BF16, name="w2_g", tag="stage", align_bytes=64)
        round_and_deal(nc.vector.tensor_copy, w2_g, w2_raw, 0, 128)
        d_bytes = keep.tile([P, H], U8, name="d_bytes", tag="w2_raw", align_bytes=64)
        nc.vector.tensor_copy(d_bytes[:].rearrange("p (t m) -> p t m", t=PACK), ds_placed[:].rearrange("p (m t) -> p t m", t=PACK))
        b_ps = [psum.tile([P, S], F32, name="b_ps%d" % t) for t in range(PACK)]
        for t in range(PACK):
            product(b_ps[t][:], (d_codes, d_bytes), t, (xw_two, xs_two), 8)
        for t in range(PACK):
            nc.vector.tensor_scalar(b_win[t][:, :S], b_ps[t][:], 0.0625, None, ALU.mult)

        w2_q = quantize(w2_g[:].rearrange("p t m j -> p (t m j)"), N, "w2", "placed")

        HALF = S // 2
        z_planes = keep.tile([P, PACK, S], F32, name="z_planes", tag="stage", align_bytes=64)

        def z_plane(t, cols):
            nc.vector.scalar_tensor_tensor(
                z_planes[:, t, cols], ds_win[t][:, cols], gn_t[:, t : t + 1], y_win[t][:, S:][:, cols], ALU.mult, ALU.mult
            )

        halves = [slice(HALF * h, HALF * (h + 1)) for h in range(2)]
        for t in range(PACK - 1):
            z_plane(t, slice(0, S))
        for cols in halves:
            z_plane(PACK - 1, cols)
        z_g = [keep.tile([P, HALF, PACK], BF16, name="z_g%d" % h, align_bytes=64) for h in range(2)]
        for h in range(2):
            nc.vector.tensor_copy(z_g[h][:], z_planes[:, :, halves[h]].rearrange("p t s -> p s t"))
        z_codes = keep.tile([P, S], U32, name="z_codes", align_bytes=64)
        z_scales = keep.tile([P, S], U8, name="z_scales", align_bytes=64)
        for h in range(2):
            nc.vector.quantize_mx(
                out=z_codes[:, halves[h]].bitcast(FP8X4), scales=z_scales[:, halves[h]], in_=z_g[h][:].rearrange("p s t -> p (s t)")
            )

        b_n4 = keep.tile([P, PACK, S], F32, name="b_n4", tag="got1", align_bytes=64)
        for t in range(PACK):
            nc.scalar.activation(b_n4[:, t, :], b_win[t][:].indirect(n4_t[:]), ACT.Copy)

        a_ps = [psum.tile([P, S], F32, name="a_ps%d" % t, tag="ya%d" % t) for t in range(PACK)]
        for t in range(PACK):
            product(a_ps[t][:], w2_q, t, (z_codes, z_scales))
        a_n3 = keep.tile([P, PACK, S], F32, name="a_n3")
        hi = keep.tile([P, PACK, S], F32, name="hi")
        lo = keep.tile([P, PACK, S], F32, name="lo")
        res = keep.tile([P, PACK, S], F32, name="res")
        out_v = out.rearrange("(p t) j -> p t j", t=PACK)
        for t in range(PACK):
            nc.vector.tensor_copy(a_win[t][:, :S], a_ps[t][:])

        def fetch_n3(t, cols):
            entries = n3_t[:, cols.start // 16 : cols.stop // 16]
            nc.scalar.activation(a_n3[:, t, cols], a_win[t][:].indirect(entries), ACT.Copy)

        def smaller(t, cols):
            nc.vector.scalar_tensor_tensor(lo[:, t, cols], b_ps[t][:, cols], 0.0625, a_n3[:, t, cols], ALU.mult, ALU.min)

        for t in range(PACK - 1):
            fetch_n3(t, slice(0, S))
            nc.vector.tensor_tensor(hi[:, t, :], a_ps[t][:], b_n4[:, t, :], ALU.max)
            smaller(t, slice(0, S))
            nc.vector.tensor_tensor(res[:, t, :], hi[:, t, :], lo[:, t, :], ALU.subtract)
            nc.sync.dma_start(out_v[:, t, :], res[:, t, :])
        t = PACK - 1
        nc.vector.tensor_tensor(hi[:, t, :], a_ps[t][:], b_n4[:, t, :], ALU.max)
        for cols in halves:
            fetch_n3(t, cols)
            smaller(t, cols)
        for cols in halves:
            nc.vector.tensor_tensor(res[:, t, cols], hi[:, t, cols], lo[:, t, cols], ALU.subtract)
        nc.sync.dma_start(out_v[:, t, :], res[:, t, :])
